import numpy as np
import ml_dtypes


def mxq(x, axis, fmt="e4m3"):
    dtype, down = {"e4m3": (ml_dtypes.float8_e4m3fn, 7), "e5m2": (ml_dtypes.float8_e5m2, 14)}[fmt]
    v = np.moveaxis(np.asarray(x, np.float32).astype(ml_dtypes.bfloat16).astype(np.float64), axis, -1)
    blocks = v.reshape(v.shape[:-1] + (-1, 32))
    amax = np.abs(blocks).max(-1, keepdims=True)
    byte = np.maximum(np.where(amax > 0, np.frexp(amax)[1] - 1 + 127, 0) - down, 1)
    scale = np.exp2(byte - 127.0)
    codes = (blocks / scale).astype(np.float32).astype(dtype).astype(np.float64)
    return np.moveaxis((codes * scale).reshape(v.shape), -1, axis)


WIDE = False


def mx_kscale(k):
    if not WIDE:
        return np.ones(k)
    levels = np.array([10, -10, 5, -5, 0])
    if k % 512:
        return np.exp2(np.random.permutation(np.resize(levels, k // 32))).repeat(32)
    a = np.empty((k // 512, 16))
    for p in range(k // 512):
        a[p, :8] = np.random.permutation(np.resize(levels, 8))
        for g in range(8):
            far = levels[np.abs(levels - a[p, g]) >= 10]
            a[p, g + 8] = far[np.random.randint(len(far))]
    return np.exp2(a.ravel()).repeat(32)


def f64(x):
    return np.asarray(x).astype(np.float64)


def striped(idx):
    return np.tile(idx.reshape(-1, 16).T, (8, 1)).astype(np.uint16)


def unstriped(offs):
    return offs[:16].T.reshape(-1).astype(np.int64)


def pack_weight(w):
    k, n = w.shape
    w = f64(np.asarray(w, np.float32).astype(ml_dtypes.bfloat16)).reshape(k // 32, 32, n)
    amax = np.abs(w).max(1)
    byte = np.clip(np.where(amax > 0, np.frexp(amax)[1] - 1 + 127 - 7, 1), 1, 254)
    scaled = (w * np.exp2(127.0 - byte)[:, None, :]).reshape(k, n).astype(np.float32)
    words = np.ascontiguousarray(scaled.reshape(k // 512, 128, 4, n).transpose(0, 1, 3, 2)).astype(ml_dtypes.float8_e4m3fn).view(np.uint8)
    return words, np.ascontiguousarray(byte.astype(np.uint8).reshape(k // 512, 16, n))


def unpack_weight(words, scales):
    g, p, n, _ = words.shape
    vals = np.ascontiguousarray(words).view(ml_dtypes.float8_e4m3fn).astype(np.float64) * np.repeat(np.exp2(scales.astype(np.float64) - 127.0), 8, axis=1)[..., None]
    return vals.transpose(0, 1, 3, 2).reshape(g * 512, n)


K, T, E, C, N = 512, 512, 8, 128, 256


def by_expert(wq, xq):
    return np.concatenate([wq[e].T @ xq[:, e * C:(e + 1) * C] for e in range(E)], axis=1)


def setup_inputs():
    n = np.random.standard_normal
    s = mx_kscale(K)[:, None]
    first = np.random.permutation(np.repeat(np.arange(E), T // E))
    second = (first + 1 + np.random.permutation(np.repeat(np.arange(E - 1), -(-T // (E - 1)))[:T])) % E
    while np.bincount(second, minlength=E).max() != T // E:
        load = np.bincount(second, minlength=E); hi, lo = int(load.argmax()), int(load.argmin())
        t = np.flatnonzero((second == hi) & (first != lo))[0]; second[t] = lo
    slot_token = np.empty(E * C, np.int64); pos = np.empty((2, T), np.int64); fill = np.zeros(E, np.int64)
    place = np.stack([np.random.permutation(C) for _ in range(E)])
    for r, deal in enumerate((first, second)):
        for t in np.random.permutation(T):
            e = deal[t]; j = e * C + place[e, fill[e]]; fill[e] += 1; slot_token[j] = t; pos[r, t] = j
    g = np.random.uniform(0.2, 0.8, T)
    packed = [pack_weight(m) for m in n((E, K, N)) / np.sqrt(K) / s[None]]
    return {
        "xT": (n((K, T)) * s).astype(np.float32),
        "w_words": np.stack([m[0] for m in packed]),
        "w_scales": np.stack([m[1] for m in packed]),
        "b": (0.3 * n((N, E))).astype(np.float32),
        "gate": np.stack([np.tile(g, (N, 1)), np.tile(1.0 - g, (N, 1))]).astype(np.float32),
        "offs": striped(slot_token),
        "pos1": striped(pos[0]),
        "pos2": striped(pos[1]),
    }


def reference(xT, w_words, w_scales, b, gate, offs, pos1, pos2):
    idx = unstriped(offs)
    xq = mxq(f64(xT)[:, idx], 0, "e4m3")
    w = np.stack([unpack_weight(w_words[e], w_scales[e]) for e in range(E)])
    y = by_expert(w, xq)
    y = y + np.repeat(f64(b), C, axis=1)
    return f64(gate[0]) * y[:, unstriped(pos1)] + f64(gate[1]) * y[:, unstriped(pos2)]

@@ -1,0 +1,136 @@
+from contextlib import ExitStack
+
+import concourse.mybir as mybir
+
+FLOPS = 2 * 512 * 256 * 1024
+
+F32 = mybir.dt.float32
+BF16 = mybir.dt.bfloat16
+U32 = mybir.dt.uint32
+I32 = mybir.dt.int32
+U16 = mybir.dt.uint16
+U8 = mybir.dt.uint8
+FP8X4 = mybir.dt.float8_e4m3fn_x4
+
+P = 128
+PACK = 4
+TOKENS = 512
+EXPERTS = 8
+CAP = 128
+SLOTS = EXPERTS * CAP
+FEATURES = 256
+BLOCKS = FEATURES // P
+CHUNK = 256
+CHUNKS = SLOTS // CHUNK
+PER_CHUNK = CHUNK // CAP
+
+
+def tile_routed_moe_kernel(tc, xT, w_words, w_scales, b, gate, offs, pos1, pos2, out):
+    nc = tc.nc
+    mult = mybir.AluOpType.mult
+    add = mybir.AluOpType.add
+    identity = mybir.ActivationFunctionType.Identity
+
+    with ExitStack() as ctx:
+        lists = ctx.enter_context(tc.tile_pool(name="lists", bufs=1))
+        keep = ctx.enter_context(tc.tile_pool(name="keep", bufs=1))
+        psum = ctx.enter_context(tc.psum_pool(name="psum", bufs=1))
+
+        offs_t = lists.tile([P, SLOTS // 16], U16, name="offs_t")
+        pos1_t = lists.tile([P, TOKENS // 16], U16, name="pos1_t")
+        pos2_t = lists.tile([P, TOKENS // 16], U16, name="pos2_t")
+        nc.sync.dma_start(offs_t[:], offs)
+
+        x_rows = xT.rearrange("(p t) n -> t p n", t=PACK)
+        planes = []
+        for t in range(PACK):
+            plane = keep.tile([P, TOKENS], F32, name="plane%d" % t)
+            nc.sync.dma_start(plane[:], x_rows[t])
+            planes.append(plane)
+
+        w_sc = keep.tile([P, EXPERTS, FEATURES], U8, name="w_sc", align_bytes=64)
+        nc.vector.memset(w_sc[:].rearrange("p e n -> p (e n)").bitcast(I32), 0)
+        sc_rows = w_scales.rearrange("e a (q r) n -> r q (e a) n", r=4)
+        for r in range(4):
+            nc.sync.dma_start(w_sc[r:P:32, :, :].bitcast(I32), sc_rows[r].bitcast(I32))
+
+        w_codes = []
+        for e in range(EXPERTS):
+            wc = keep.tile([P, FEATURES], I32, name="w_codes%d" % e, align_bytes=64)
+            nc.sync.dma_start(wc[:], w_words[e, 0].rearrange("p n r -> p (n r)").bitcast(I32))
+            w_codes.append(wc)
+
+        nc.sync.dma_start(pos1_t[:], pos1)
+        nc.sync.dma_start(pos2_t[:], pos2)
+        bias_t = keep.tile([P, BLOCKS, EXPERTS], F32, name="bias_t")
+        nc.sync.dma_start(bias_t[:], b.rearrange("(h p) e -> p h e", p=P))
+        gates = {}
+        for h in range(BLOCKS):
+            for r in range(2):
+                g = keep.tile([P, TOKENS], F32, name="gate%d_%d" % (r, h))
+                nc.sync.dma_start(g[:], gate[r, h * P:(h + 1) * P, :])
+                gates[(r, h)] = g
+
+        y = [keep.tile([P, SLOTS], F32, name="y%d" % h) for h in range(BLOCKS)]
+
+        gathered = {}
+        grouped = {}
+
+        def gather(c):
+            g4 = keep.tile([P, PACK, CHUNK], F32, name="g4_%d" % c)
+            cols = offs_t[:, c * (CHUNK // 16):(c + 1) * (CHUNK // 16)]
+            for t in range(PACK):
+                nc.vector.tensor_copy(g4[:, t, :], planes[t][:].indirect(cols))
+            gathered[c] = g4
+
+        def interleave(c):
+            gr = keep.tile([P, CHUNK, PACK], BF16, name="grouped%d" % c, align_bytes=64)
+            nc.scalar.copy(gr[:], gathered[c][:].rearrange("p t n -> p n t"))
+            grouped[c] = gr
+
+        def multiply(c):
+            xc = keep.tile([P, CHUNK], U32, name="x_codes%d" % c, align_bytes=64)
+            xs = keep.tile([P, CHUNK], U8, name="x_sc%d" % c, align_bytes=64)
+            nc.vector.quantize_mx(
+                out=xc[:].bitcast(FP8X4),
+                scales=xs[:],
+                in_=grouped[c][:].rearrange("p n t -> p (n t)"),
+            )
+            for h in range(BLOCKS):
+                acc = psum.tile([P, CHUNK], F32, name="acc%d_%d" % (h, c))
+                for i in range(PER_CHUNK):
+                    e = c * PER_CHUNK + i
+                    nc.tensor.matmul_mx(
+                        out=acc[:, i * CAP:(i + 1) * CAP],
+                        lhsT=w_codes[e][:, h * P:(h + 1) * P].bitcast(FP8X4),
+                        lhsT_scale=w_sc[:, e, h * P:(h + 1) * P],
+                        rhs=xc[:, i * CAP:(i + 1) * CAP].bitcast(FP8X4),
+                        rhs_scale=xs[:, i * CAP:(i + 1) * CAP],
+                        start=True,
+                        stop=True,
+                    )
+                for i in range(PER_CHUNK):
+                    e = c * PER_CHUNK + i
+                    nc.scalar.activation(
+                        out=y[h][:, e * CAP:(e + 1) * CAP],
+                        in_=acc[:, i * CAP:(i + 1) * CAP],
+                        func=identity,
+                        bias=bias_t[:, h, e:e + 1],
+                        scale=1.0,
+                    )
+
+        for c in range(CHUNKS):
+            gather(c)
+            interleave(c)
+            if c >= 1:
+                multiply(c - 1)
+        multiply(CHUNKS - 1)
+
+        for h in range(BLOCKS):
+            first = keep.tile([P, TOKENS], F32, name="first%d" % h)
+            second = keep.tile([P, TOKENS], F32, name="second%d" % h)
+            nc.vector.tensor_tensor(first[:], y[h][:].indirect(pos1_t[:]), gates[(0, h)][:], mult)
+            nc.vector.tensor_tensor(second[:], y[h][:].indirect(pos2_t[:]), gates[(1, h)][:], mult)
+            total = keep.tile([P, TOKENS], F32, name="total%d" % h)
+            nc.vector.tensor_tensor(total[:], first[:], second[:], add)
+            nc.sync.dma_start(out[h * P:(h + 1) * P, :], total[:])

@@ -13,16 +13,15 @@ U8 = mybir.dt.uint8
 FP8X4 = mybir.dt.float8_e4m3fn_x4
 
 P = 128
-PACK = 4
 TOKENS = 512
 EXPERTS = 8
 CAP = 128
 SLOTS = EXPERTS * CAP
 FEATURES = 256
 BLOCKS = FEATURES // P
-CHUNK = 256
-CHUNKS = SLOTS // CHUNK
-PER_CHUNK = CHUNK // CAP
+PACK = 4
+VEC_PLANES = 3
+SIZES = [256,256,256,256]
 
 
 def tile_routed_moe_kernel(tc, xT, w_words, w_scales, b, gate, offs, pos1, pos2, out):
@@ -30,10 +29,12 @@ def tile_routed_moe_kernel(tc, xT, w_words, w_scales, b, gate, offs, pos1, pos2,
     mult = mybir.AluOpType.mult
     add = mybir.AluOpType.add
     identity = mybir.ActivationFunctionType.Identity
+    copy = mybir.ActivationFunctionType.Copy
 
     with ExitStack() as ctx:
         lists = ctx.enter_context(tc.tile_pool(name="lists", bufs=1))
         keep = ctx.enter_context(tc.tile_pool(name="keep", bufs=1))
+        ring = ctx.enter_context(tc.tile_pool(name="ring", bufs=3))
         psum = ctx.enter_context(tc.psum_pool(name="psum", bufs=1))
 
         offs_t = lists.tile([P, SLOTS // 16], U16, name="offs_t")
@@ -42,11 +43,11 @@ def tile_routed_moe_kernel(tc, xT, w_words, w_scales, b, gate, offs, pos1, pos2,
         nc.sync.dma_start(offs_t[:], offs)
 
         x_rows = xT.rearrange("(p t) n -> t p n", t=PACK)
-        planes = []
-        for t in range(PACK):
+        planes = {}
+        for t in [0,3,1,2]:
             plane = keep.tile([P, TOKENS], F32, name="plane%d" % t)
             nc.sync.dma_start(plane[:], x_rows[t])
-            planes.append(plane)
+            planes[t] = plane
 
         w_sc = keep.tile([P, EXPERTS, FEATURES], U8, name="w_sc", align_bytes=64)
         nc.vector.memset(w_sc[:].rearrange("p e n -> p (e n)").bitcast(I32), 0)
@@ -72,65 +73,101 @@ def tile_routed_moe_kernel(tc, xT, w_words, w_scales, b, gate, offs, pos1, pos2,
                 gates[(r, h)] = g
 
         y = [keep.tile([P, SLOTS], F32, name="y%d" % h) for h in range(BLOCKS)]
-
+        starts = [sum(SIZES[:c]) for c in range(len(SIZES))]
         gathered = {}
-        grouped = {}
+        codes = {}
+        banks = {}
+        for h in range(BLOCKS):
+            for pair in range(EXPERTS // 2):
+                banks[(h, pair)] = psum.tile([P, 2 * CAP], F32, name="bank%d_%d" % (h, pair))
+        grouped = [keep.tile([P, SIZES[c], PACK], BF16, name="grouped%d" % c, align_bytes=64) for c in range(len(SIZES))]
+
+        xb = keep.tile([P, 2, TOKENS], BF16, name="xb")
+        nc.scalar.copy(xb[:, 0, :], planes[3][:])
 
         def gather(c):
-            g4 = keep.tile([P, PACK, CHUNK], F32, name="g4_%d" % c)
-            cols = offs_t[:, c * (CHUNK // 16):(c + 1) * (CHUNK // 16)]
-            for t in range(PACK):
-                nc.vector.tensor_copy(g4[:, t, :], planes[t][:].indirect(cols))
-            gathered[c] = g4
+            n = SIZES[c]
+            g3 = ring.tile([P, VEC_PLANES, n], F32, name="g3")
+            cols = offs_t[:, starts[c] // 16:(starts[c] + n) // 16]
+            for t in range(VEC_PLANES):
+                nc.vector.tensor_copy(g3[:, t, :], planes[t][:].indirect(cols))
+            gathered[c] = g3
+
+        def scalar_gather(c):
+            for i in range(SIZES[c] // CAP):
+                e = starts[c] // CAP + i
+                nc.scalar.activation(
+                    grouped[c][:, i * CAP:(i + 1) * CAP, 3],
+                    xb[:, 0, :].indirect(offs_t[:, e * (CAP // 16):(e + 1) * (CAP // 16)]),
+                    copy,
+                )
 
         def interleave(c):
-            gr = keep.tile([P, CHUNK, PACK], BF16, name="grouped%d" % c, align_bytes=64)
-            nc.scalar.copy(gr[:], gathered[c][:].rearrange("p t n -> p n t"))
-            grouped[c] = gr
+            nc.scalar.copy(grouped[c][:, :, 0:VEC_PLANES], gathered[c][:].rearrange("p t n -> p n t"))
 
-        def multiply(c):
-            xc = keep.tile([P, CHUNK], U32, name="x_codes%d" % c, align_bytes=64)
-            xs = keep.tile([P, CHUNK], U8, name="x_sc%d" % c, align_bytes=64)
-            nc.vector.quantize_mx(
-                out=xc[:].bitcast(FP8X4),
-                scales=xs[:],
-                in_=grouped[c][:].rearrange("p n t -> p (n t)"),
-            )
-            for h in range(BLOCKS):
-                acc = psum.tile([P, CHUNK], F32, name="acc%d_%d" % (h, c))
-                for i in range(PER_CHUNK):
-                    e = c * PER_CHUNK + i
-                    nc.tensor.matmul_mx(
-                        out=acc[:, i * CAP:(i + 1) * CAP],
-                        lhsT=w_codes[e][:, h * P:(h + 1) * P].bitcast(FP8X4),
-                        lhsT_scale=w_sc[:, e, h * P:(h + 1) * P],
-                        rhs=xc[:, i * CAP:(i + 1) * CAP].bitcast(FP8X4),
-                        rhs_scale=xs[:, i * CAP:(i + 1) * CAP],
-                        start=True,
-                        stop=True,
-                    )
-                for i in range(PER_CHUNK):
-                    e = c * PER_CHUNK + i
-                    nc.scalar.activation(
-                        out=y[h][:, e * CAP:(e + 1) * CAP],
-                        in_=acc[:, i * CAP:(i + 1) * CAP],
-                        func=identity,
-                        bias=bias_t[:, h, e:e + 1],
-                        scale=1.0,
-                    )
+        def quantize(c):
+            n = SIZES[c]
+            xc = keep.tile([P, n], U32, name="x_codes%d" % c, align_bytes=64)
+            xs = keep.tile([P, n], U8, name="x_sc%d" % c, align_bytes=64)
+            nc.vector.quantize_mx(out=xc[:].bitcast(FP8X4), scales=xs[:], in_=grouped[c][:].rearrange("p n t -> p (n t)"))
+            codes[c] = (xc, xs)
 
-        for c in range(CHUNKS):
+        def multiply(c, h):
+            n = SIZES[c]
+            xc, xs = codes[c]
+            for i in range(n // CAP):
+                e = starts[c] // CAP + i
+                nc.tensor.matmul_mx(
+                    out=banks[(h, e // 2)][:, (e % 2) * CAP:(e % 2 + 1) * CAP],
+                    lhsT=w_codes[e][:, h * P:(h + 1) * P].bitcast(FP8X4),
+                    lhsT_scale=w_sc[:, e, h * P:(h + 1) * P],
+                    rhs=xc[:, i * CAP:(i + 1) * CAP].bitcast(FP8X4),
+                    rhs_scale=xs[:, i * CAP:(i + 1) * CAP],
+                    start=True,
+                    stop=True,
+                )
+
+        def empty(c, h):
+            for i in range(SIZES[c] // CAP):
+                e = starts[c] // CAP + i
+                nc.scalar.activation(
+                    out=y[h][:, e * CAP:(e + 1) * CAP],
+                    in_=banks[(h, e // 2)][:, (e % 2) * CAP:(e % 2 + 1) * CAP],
+                    func=identity,
+                    bias=bias_t[:, h, e:e + 1],
+                    scale=1.0,
+                )
+
+        def after(c):
+            quantize(c)
+            multiply(c, 0)
+            empty(c, 0)
+            multiply(c, 1)
+
+        for c in range(len(SIZES)):
+            scalar_gather(c)
+        for c in range(len(SIZES)):
             gather(c)
             interleave(c)
-            if c >= 1:
-                multiply(c - 1)
-        multiply(CHUNKS - 1)
+        for c in range(len(SIZES)):
+            after(c)
+        for c in range(len(SIZES)):
+            empty(c, 1)
 
-        for h in range(BLOCKS):
-            first = keep.tile([P, TOKENS], F32, name="first%d" % h)
-            second = keep.tile([P, TOKENS], F32, name="second%d" % h)
-            nc.vector.tensor_tensor(first[:], y[h][:].indirect(pos1_t[:]), gates[(0, h)][:], mult)
-            nc.vector.tensor_tensor(second[:], y[h][:].indirect(pos2_t[:]), gates[(1, h)][:], mult)
-            total = keep.tile([P, TOKENS], F32, name="total%d" % h)
-            nc.vector.tensor_tensor(total[:], first[:], second[:], add)
-            nc.sync.dma_start(out[h * P:(h + 1) * P, :], total[:])
+        first = [keep.tile([P, TOKENS], F32, name="first%d" % h) for h in range(BLOCKS)]
+        second = [keep.tile([P, TOKENS], F32, name="second%d" % h) for h in range(BLOCKS)]
+        total = [keep.tile([P, TOKENS], F32, name="total%d" % h) for h in range(BLOCKS)]
+
+        def fetch(dst, h, r, pos_t):
+            nc.vector.tensor_tensor(dst[h][:], y[h][:].indirect(pos_t[:]), gates[(r, h)][:], mult)
+
+        def finish(h):
+            nc.vector.tensor_tensor(total[h][:], first[h][:], second[h][:], add)
+            nc.sync.dma_start(out[h * P:(h + 1) * P, :], total[h][:])
+
+        fetch(first, 0, 0, pos1_t)
+        fetch(second, 0, 1, pos2_t)
+        fetch(first, 1, 0, pos1_t)
+        finish(0)
+        fetch(second, 1, 1, pos2_t)
+        finish(1)

@@ -37,6 +37,10 @@ def tile_routed_moe_kernel(tc, xT, w_words, w_scales, b, gate, offs, pos1, pos2,
         ring = ctx.enter_context(tc.tile_pool(name="ring", bufs=3))
         psum = ctx.enter_context(tc.psum_pool(name="psum", bufs=1))
 
+        warm = keep.tile([P, 2], F32, name="warm")
+        nc.vector.memset(warm[:, 0:1], 0.0)
+        nc.scalar.activation(out=warm[:, 1:2], in_=warm[:, 0:1], func=copy)
+
         offs_t = lists.tile([P, SLOTS // 16], U16, name="offs_t")
         pos1_t = lists.tile([P, TOKENS // 16], U16, name="pos1_t")
         pos2_t = lists.tile([P, TOKENS // 16], U16, name="pos2_t")

@@ -20,8 +20,7 @@ SLOTS = EXPERTS * CAP
 FEATURES = 256
 BLOCKS = FEATURES // P
 PACK = 4
-VEC_PLANES = 3
-SIZES = [256,256,256,256]
+CHUNKS = [(256, 2), (256, 2), (256, 2), (256, 2)]
 
 
 def tile_routed_moe_kernel(tc, xT, w_words, w_scales, b, gate, offs, pos1, pos2, out):
@@ -34,7 +33,7 @@ def tile_routed_moe_kernel(tc, xT, w_words, w_scales, b, gate, offs, pos1, pos2,
     with ExitStack() as ctx:
         lists = ctx.enter_context(tc.tile_pool(name="lists", bufs=1))
         keep = ctx.enter_context(tc.tile_pool(name="keep", bufs=1))
-        ring = ctx.enter_context(tc.tile_pool(name="ring", bufs=3))
+        ring = ctx.enter_context(tc.tile_pool(name="ring", bufs=4))
         psum = ctx.enter_context(tc.psum_pool(name="psum", bufs=1))
 
         warm = keep.tile([P, 2], F32, name="warm")
@@ -48,7 +47,7 @@ def tile_routed_moe_kernel(tc, xT, w_words, w_scales, b, gate, offs, pos1, pos2,
 
         x_rows = xT.rearrange("(p t) n -> t p n", t=PACK)
         planes = {}
-        for t in [0,3,1,2]:
+        for t in [2,0,3,1]:
             plane = keep.tile([P, TOKENS], F32, name="plane%d" % t)
             nc.sync.dma_start(plane[:], x_rows[t])
             planes[t] = plane
@@ -77,49 +76,63 @@ def tile_routed_moe_kernel(tc, xT, w_words, w_scales, b, gate, offs, pos1, pos2,
                 gates[(r, h)] = g
 
         y = [keep.tile([P, SLOTS], F32, name="y%d" % h) for h in range(BLOCKS)]
-        starts = [sum(SIZES[:c]) for c in range(len(SIZES))]
+        sizes = [n for n, vp in CHUNKS]
+        starts = [sum(sizes[:c]) for c in range(len(CHUNKS))]
         gathered = {}
         codes = {}
         banks = {}
         for h in range(BLOCKS):
             for pair in range(EXPERTS // 2):
                 banks[(h, pair)] = psum.tile([P, 2 * CAP], F32, name="bank%d_%d" % (h, pair))
-        grouped = [keep.tile([P, SIZES[c], PACK], BF16, name="grouped%d" % c, align_bytes=64) for c in range(len(SIZES))]
+        grouped = [keep.tile([P, sizes[c], PACK], BF16, name="grouped%d" % c, align_bytes=64) for c in range(len(CHUNKS))]
 
         xb = keep.tile([P, 2, TOKENS], BF16, name="xb")
-        nc.scalar.copy(xb[:, 0, :], planes[3][:])
+        for t in [2,3]:
+            if t == 2:
+                nc.scalar.copy(xb[:, t - 2, :], planes[t][:])
+            else:
+                nc.gpsimd.tensor_scalar(out=xb[:, t - 2, :], in0=planes[t][:], scalar1=1.0, scalar2=0.0, op0=mult, op1=add)
 
         def gather(c):
-            n = SIZES[c]
-            g3 = ring.tile([P, VEC_PLANES, n], F32, name="g3")
+            n, vp = CHUNKS[c]
+            gt = ring.tile([P, vp, n], F32, name="gt")
             cols = offs_t[:, starts[c] // 16:(starts[c] + n) // 16]
-            for t in range(VEC_PLANES):
-                nc.vector.tensor_copy(g3[:, t, :], planes[t][:].indirect(cols))
-            gathered[c] = g3
+            for t in range(vp):
+                nc.vector.tensor_copy(gt[:, t, :], planes[t][:].indirect(cols))
+            gathered[c] = gt
 
         def scalar_gather(c):
-            for i in range(SIZES[c] // CAP):
+            n, vp = CHUNKS[c]
+            for i in range(n // CAP):
                 e = starts[c] // CAP + i
-                nc.scalar.activation(
-                    grouped[c][:, i * CAP:(i + 1) * CAP, 3],
-                    xb[:, 0, :].indirect(offs_t[:, e * (CAP // 16):(e + 1) * (CAP // 16)]),
-                    copy,
-                )
+                for t in range(vp, PACK):
+                    nc.scalar.activation(
+                        grouped[c][:, i * CAP:(i + 1) * CAP, t],
+                        xb[:, t - 2, :].indirect(offs_t[:, e * (CAP // 16):(e + 1) * (CAP // 16)]),
+                        copy,
+                    )
 
         def interleave(c):
-            nc.scalar.copy(grouped[c][:, :, 0:VEC_PLANES], gathered[c][:].rearrange("p t n -> p n t"))
+            n, vp = CHUNKS[c]
+            nc.gpsimd.tensor_scalar(
+                out=grouped[c][:, :, 0:vp],
+                in0=gathered[c][:].rearrange("p t n -> p n t"),
+                scalar1=1.0,
+                scalar2=0.0,
+                op0=mult,
+                op1=add,
+            )
 
         def quantize(c):
-            n = SIZES[c]
+            n = sizes[c]
             xc = keep.tile([P, n], U32, name="x_codes%d" % c, align_bytes=64)
             xs = keep.tile([P, n], U8, name="x_sc%d" % c, align_bytes=64)
             nc.vector.quantize_mx(out=xc[:].bitcast(FP8X4), scales=xs[:], in_=grouped[c][:].rearrange("p n t -> p (n t)"))
             codes[c] = (xc, xs)
 
         def multiply(c, h):
-            n = SIZES[c]
             xc, xs = codes[c]
-            for i in range(n // CAP):
+            for i in range(sizes[c] // CAP):
                 e = starts[c] // CAP + i
                 nc.tensor.matmul_mx(
                     out=banks[(h, e // 2)][:, (e % 2) * CAP:(e % 2 + 1) * CAP],
@@ -132,7 +145,7 @@ def tile_routed_moe_kernel(tc, xT, w_words, w_scales, b, gate, offs, pos1, pos2,
                 )
 
         def empty(c, h):
-            for i in range(SIZES[c] // CAP):
+            for i in range(sizes[c] // CAP):
                 e = starts[c] // CAP + i
                 nc.scalar.activation(
                     out=y[h][:, e * CAP:(e + 1) * CAP],
@@ -142,20 +155,17 @@ def tile_routed_moe_kernel(tc, xT, w_words, w_scales, b, gate, offs, pos1, pos2,
                     scale=1.0,
                 )
 
-        def after(c):
+        for c in range(len(CHUNKS)):
+            scalar_gather(c)
+        for c in range(len(CHUNKS)):
+            gather(c)
+            interleave(c)
+        for c in range(len(CHUNKS)):
             quantize(c)
             multiply(c, 0)
             empty(c, 0)
             multiply(c, 1)
-
-        for c in range(len(SIZES)):
-            scalar_gather(c)
-        for c in range(len(SIZES)):
-            gather(c)
-            interleave(c)
-        for c in range(len(SIZES)):
-            after(c)
-        for c in range(len(SIZES)):
+        for c in range(len(CHUNKS)):
             empty(c, 1)
 
         first = [keep.tile([P, TOKENS], F32, name="first%d" % h) for h in range(BLOCKS)]

@@ -20,7 +20,9 @@ SLOTS = EXPERTS * CAP
 FEATURES = 256
 BLOCKS = FEATURES // P
 PACK = 4
-CHUNKS = [(256, 2), (256, 2), (256, 2), (256, 2)]
+QCH = [512,256,128,128]
+GCH = [256,256,256,256]
+V_EMPTIES = [4,5]
 
 
 def tile_routed_moe_kernel(tc, xT, w_words, w_scales, b, gate, offs, pos1, pos2, out):
@@ -33,7 +35,7 @@ def tile_routed_moe_kernel(tc, xT, w_words, w_scales, b, gate, offs, pos1, pos2,
     with ExitStack() as ctx:
         lists = ctx.enter_context(tc.tile_pool(name="lists", bufs=1))
         keep = ctx.enter_context(tc.tile_pool(name="keep", bufs=1))
-        ring = ctx.enter_context(tc.tile_pool(name="ring", bufs=4))
+        ring = ctx.enter_context(tc.tile_pool(name="ring", bufs=3))
         psum = ctx.enter_context(tc.psum_pool(name="psum", bufs=1))
 
         warm = keep.tile([P, 2], F32, name="warm")
@@ -43,26 +45,34 @@ def tile_routed_moe_kernel(tc, xT, w_words, w_scales, b, gate, offs, pos1, pos2,
         offs_t = lists.tile([P, SLOTS // 16], U16, name="offs_t")
         pos1_t = lists.tile([P, TOKENS // 16], U16, name="pos1_t")
         pos2_t = lists.tile([P, TOKENS // 16], U16, name="pos2_t")
-        nc.sync.dma_start(offs_t[:], offs)
 
         x_rows = xT.rearrange("(p t) n -> t p n", t=PACK)
         planes = {}
-        for t in [2,0,3,1]:
+        for i, t in enumerate([2,0,3,1]):
             plane = keep.tile([P, TOKENS], F32, name="plane%d" % t)
             nc.sync.dma_start(plane[:], x_rows[t])
             planes[t] = plane
+            if i == 0:
+                nc.sync.dma_start(offs_t[:], offs)
 
         w_sc = keep.tile([P, EXPERTS, FEATURES], U8, name="w_sc", align_bytes=64)
         nc.vector.memset(w_sc[:].rearrange("p e n -> p (e n)").bitcast(I32), 0)
         sc_rows = w_scales.rearrange("e a (q r) n -> r q (e a) n", r=4)
-        for r in range(4):
-            nc.sync.dma_start(w_sc[r:P:32, :, :].bitcast(I32), sc_rows[r].bitcast(I32))
+
+        def load_scales():
+            for r in range(4):
+                nc.sync.dma_start(w_sc[r:P:32, :, :].bitcast(I32), sc_rows[r].bitcast(I32))
 
         w_codes = []
-        for e in range(EXPERTS):
-            wc = keep.tile([P, FEATURES], I32, name="w_codes%d" % e, align_bytes=64)
-            nc.sync.dma_start(wc[:], w_words[e, 0].rearrange("p n r -> p (n r)").bitcast(I32))
-            w_codes.append(wc)
+
+        def load_codes():
+            for e in range(EXPERTS):
+                wc = keep.tile([P, FEATURES], I32, name="w_codes%d" % e, align_bytes=64)
+                nc.sync.dma_start(wc[:], w_words[e, 0].rearrange("p n r -> p (n r)").bitcast(I32))
+                w_codes.append(wc)
+
+        load_scales()
+        load_codes()
 
         nc.sync.dma_start(pos1_t[:], pos1)
         nc.sync.dma_start(pos2_t[:], pos2)
@@ -76,55 +86,55 @@ def tile_routed_moe_kernel(tc, xT, w_words, w_scales, b, gate, offs, pos1, pos2,
                 gates[(r, h)] = g
 
         y = [keep.tile([P, SLOTS], F32, name="y%d" % h) for h in range(BLOCKS)]
-        sizes = [n for n, vp in CHUNKS]
-        starts = [sum(sizes[:c]) for c in range(len(CHUNKS))]
+        qstart = [sum(QCH[:c]) for c in range(len(QCH))]
+        gstart = [sum(GCH[:c]) for c in range(len(GCH))]
         gathered = {}
         codes = {}
         banks = {}
-        for h in range(BLOCKS):
-            for pair in range(EXPERTS // 2):
-                banks[(h, pair)] = psum.tile([P, 2 * CAP], F32, name="bank%d_%d" % (h, pair))
-        grouped = [keep.tile([P, sizes[c], PACK], BF16, name="grouped%d" % c, align_bytes=64) for c in range(len(CHUNKS))]
+        grouped = [keep.tile([P, QCH[c], PACK], BF16, name="grouped%d" % c, align_bytes=64) for c in range(len(QCH))]
+
+        def where(slot):
+            c = max(i for i in range(len(QCH)) if qstart[i] <= slot)
+            return c, slot - qstart[c]
 
         xb = keep.tile([P, 2, TOKENS], BF16, name="xb")
-        for t in [2,3]:
-            if t == 2:
-                nc.scalar.copy(xb[:, t - 2, :], planes[t][:])
-            else:
-                nc.gpsimd.tensor_scalar(out=xb[:, t - 2, :], in0=planes[t][:], scalar1=1.0, scalar2=0.0, op0=mult, op1=add)
+        nc.vector.tensor_copy(xb[:, 0, :], planes[2][:])
+        nc.gpsimd.tensor_scalar(out=xb[:, 1, :], in0=planes[3][:], scalar1=1.0, scalar2=0.0, op0=mult, op1=add)
 
-        def gather(c):
-            n, vp = CHUNKS[c]
-            gt = ring.tile([P, vp, n], F32, name="gt")
-            cols = offs_t[:, starts[c] // 16:(starts[c] + n) // 16]
-            for t in range(vp):
+        def gather(g):
+            n = GCH[g]
+            gt = ring.tile([P, 2, n], F32, name="gt")
+            cols = offs_t[:, gstart[g] // 16:(gstart[g] + n) // 16]
+            for t in range(2):
                 nc.vector.tensor_copy(gt[:, t, :], planes[t][:].indirect(cols))
-            gathered[c] = gt
+            gathered[g] = gt
 
-        def scalar_gather(c):
-            n, vp = CHUNKS[c]
-            for i in range(n // CAP):
-                e = starts[c] // CAP + i
-                for t in range(vp, PACK):
-                    nc.scalar.activation(
-                        grouped[c][:, i * CAP:(i + 1) * CAP, t],
-                        xb[:, t - 2, :].indirect(offs_t[:, e * (CAP // 16):(e + 1) * (CAP // 16)]),
-                        copy,
-                    )
+        def scalar_gather(e):
+            c, o = where(e * CAP)
+            for t in (2, 3):
+                nc.scalar.activation(
+                    grouped[c][:, o:o + CAP, t],
+                    xb[:, t - 2, :].indirect(offs_t[:, e * (CAP // 16):(e + 1) * (CAP // 16)]),
+                    copy,
+                )
 
-        def interleave(c):
-            n, vp = CHUNKS[c]
-            nc.gpsimd.tensor_scalar(
-                out=grouped[c][:, :, 0:vp],
-                in0=gathered[c][:].rearrange("p t n -> p n t"),
-                scalar1=1.0,
-                scalar2=0.0,
-                op0=mult,
-                op1=add,
-            )
+        def interleave(g):
+            lo = gstart[g]
+            while lo < gstart[g] + GCH[g]:
+                c, o = where(lo)
+                n = min(QCH[c] - o, gstart[g] + GCH[g] - lo)
+                nc.gpsimd.tensor_scalar(
+                    out=grouped[c][:, o:o + n, 0:2],
+                    in0=gathered[g][:, :, lo - gstart[g]:lo - gstart[g] + n].rearrange("p t n -> p n t"),
+                    scalar1=1.0,
+                    scalar2=0.0,
+                    op0=mult,
+                    op1=add,
+                )
+                lo += n
 
         def quantize(c):
-            n = sizes[c]
+            n = QCH[c]
             xc = keep.tile([P, n], U32, name="x_codes%d" % c, align_bytes=64)
             xs = keep.tile([P, n], U8, name="x_sc%d" % c, align_bytes=64)
             nc.vector.quantize_mx(out=xc[:].bitcast(FP8X4), scales=xs[:], in_=grouped[c][:].rearrange("p n t -> p (n t)"))
@@ -132,10 +142,11 @@ def tile_routed_moe_kernel(tc, xT, w_words, w_scales, b, gate, offs, pos1, pos2,
 
         def multiply(c, h):
             xc, xs = codes[c]
-            for i in range(sizes[c] // CAP):
-                e = starts[c] // CAP + i
+            banks[(h, c)] = psum.tile([P, QCH[c]], F32, name="bank%d" % c)
+            for i in range(QCH[c] // CAP):
+                e = qstart[c] // CAP + i
                 nc.tensor.matmul_mx(
-                    out=banks[(h, e // 2)][:, (e % 2) * CAP:(e % 2 + 1) * CAP],
+                    out=banks[(h, c)][:, i * CAP:(i + 1) * CAP],
                     lhsT=w_codes[e][:, h * P:(h + 1) * P].bitcast(FP8X4),
                     lhsT_scale=w_sc[:, e, h * P:(h + 1) * P],
                     rhs=xc[:, i * CAP:(i + 1) * CAP].bitcast(FP8X4),
@@ -145,39 +156,48 @@ def tile_routed_moe_kernel(tc, xT, w_words, w_scales, b, gate, offs, pos1, pos2,
                 )
 
         def empty(c, h):
-            for i in range(sizes[c] // CAP):
-                e = starts[c] // CAP + i
-                nc.scalar.activation(
-                    out=y[h][:, e * CAP:(e + 1) * CAP],
-                    in_=banks[(h, e // 2)][:, (e % 2) * CAP:(e % 2 + 1) * CAP],
-                    func=identity,
-                    bias=bias_t[:, h, e:e + 1],
-                    scale=1.0,
-                )
+            for i in range(QCH[c] // CAP):
+                e = qstart[c] // CAP + i
+                if h == 0 and e in V_EMPTIES:
+                    nc.vector.tensor_scalar(
+                        out=y[h][:, e * CAP:(e + 1) * CAP],
+                        in0=banks[(h, c)][:, i * CAP:(i + 1) * CAP],
+                        scalar1=bias_t[:, h, e:e + 1],
+                        scalar2=None,
+                        op0=add,
+                    )
+                else:
+                    nc.scalar.activation(
+                        out=y[h][:, e * CAP:(e + 1) * CAP],
+                        in_=banks[(h, c)][:, i * CAP:(i + 1) * CAP],
+                        func=identity,
+                        bias=bias_t[:, h, e:e + 1],
+                        scale=1.0,
+                    )
 
-        for c in range(len(CHUNKS)):
-            scalar_gather(c)
-        for c in range(len(CHUNKS)):
-            gather(c)
-            interleave(c)
-        for c in range(len(CHUNKS)):
+        for e in range(EXPERTS):
+            scalar_gather(e)
+        for g in range(len(GCH)):
+            gather(g)
+            interleave(g)
+        for c in range(len(QCH)):
             quantize(c)
             multiply(c, 0)
             empty(c, 0)
+        for c in range(len(QCH)):
             multiply(c, 1)
-        for c in range(len(CHUNKS)):
             empty(c, 1)
 
         first = [keep.tile([P, TOKENS], F32, name="first%d" % h) for h in range(BLOCKS)]
         second = [keep.tile([P, TOKENS], F32, name="second%d" % h) for h in range(BLOCKS)]
         total = [keep.tile([P, TOKENS], F32, name="total%d" % h) for h in range(BLOCKS)]
 
-        def fetch(dst, h, r, pos_t):
-            nc.vector.tensor_tensor(dst[h][:], y[h][:].indirect(pos_t[:]), gates[(r, h)][:], mult)
+        def fetch(dst, h, r, pos_t, lo=0, hi=TOKENS):
+            nc.vector.tensor_tensor(dst[h][:, lo:hi], y[h][:].indirect(pos_t[:, lo // 16:hi // 16]), gates[(r, h)][:, lo:hi], mult)
 
-        def finish(h):
-            nc.vector.tensor_tensor(total[h][:], first[h][:], second[h][:], add)
-            nc.sync.dma_start(out[h * P:(h + 1) * P, :], total[h][:])
+        def finish(h, lo=0, hi=TOKENS):
+            nc.vector.tensor_tensor(total[h][:, lo:hi], first[h][:, lo:hi], second[h][:, lo:hi], add)
+            nc.sync.dma_start(out[h * P:(h + 1) * P, lo:hi], total[h][:, lo:hi])
 
         fetch(first, 0, 0, pos1_t)
         fetch(second, 0, 1, pos2_t)

@@ -1,6 +1,7 @@
 from contextlib import ExitStack
 
 import concourse.mybir as mybir
+from concourse.masks import make_identity
 
 FLOPS = 2 * 512 * 256 * 1024
 
@@ -41,6 +42,9 @@ def tile_routed_moe_kernel(tc, xT, w_words, w_scales, b, gate, offs, pos1, pos2,
         warm = keep.tile([P, 2], F32, name="warm")
         nc.vector.memset(warm[:, 0:1], 0.0)
         nc.scalar.activation(out=warm[:, 1:2], in_=warm[:, 0:1], func=copy)
+
+        ident = keep.tile([P, P], F32, name="ident")
+        make_identity(nc, ident[:])
 
         offs_t = lists.tile([P, SLOTS // 16], U16, name="offs_t")
         pos1_t = lists.tile([P, TOKENS // 16], U16, name="pos1_t")
@@ -199,9 +203,15 @@ def tile_routed_moe_kernel(tc, xT, w_words, w_scales, b, gate, offs, pos1, pos2,
             nc.vector.tensor_tensor(total[h][:, lo:hi], first[h][:, lo:hi], second[h][:, lo:hi], add)
             nc.sync.dma_start(out[h * P:(h + 1) * P, lo:hi], total[h][:, lo:hi])
 
+        PE_COLS = 400
+        acc = psum.tile([P, PE_COLS], F32, name="acc")
         fetch(first, 0, 0, pos1_t)
+        nc.tensor.matmul(acc[:], lhsT=ident[:], rhs=first[0][:, 0:PE_COLS], start=True, stop=False)
         fetch(second, 0, 1, pos2_t)
+        nc.tensor.matmul(acc[:], lhsT=ident[:], rhs=second[0][:, 0:PE_COLS], start=False, stop=True)
+        nc.scalar.copy(total[0][:, 0:PE_COLS], acc[:])
         fetch(first, 1, 0, pos1_t)
-        finish(0)
+        nc.vector.tensor_tensor(total[0][:, PE_COLS:TOKENS], first[0][:, PE_COLS:TOKENS], second[0][:, PE_COLS:TOKENS], add)
+        nc.sync.dma_start(out[0:P, :], total[0][:])
         fetch(second, 1, 1, pos2_t)
         finish(1)

@@ -127,14 +127,20 @@ def tile_routed_moe_kernel(tc, xT, w_words, w_scales, b, gate, offs, pos1, pos2,
             while lo < gstart[g] + GCH[g]:
                 c, o = where(lo)
                 n = min(QCH[c] - o, gstart[g] + GCH[g] - lo)
-                nc.gpsimd.tensor_scalar(
-                    out=grouped[c][:, o:o + n, 0:2],
-                    in0=gathered[g][:, :, lo - gstart[g]:lo - gstart[g] + n].rearrange("p t n -> p n t"),
-                    scalar1=1.0,
-                    scalar2=0.0,
-                    op0=mult,
-                    op1=add,
-                )
+                if c in [3]:
+                    nc.vector.tensor_copy(
+                        out=grouped[c][:, o:o + n, 0:2],
+                        in_=gathered[g][:, :, lo - gstart[g]:lo - gstart[g] + n].rearrange("p t n -> p n t"),
+                    )
+                else:
+                    nc.gpsimd.tensor_scalar(
+                        out=grouped[c][:, o:o + n, 0:2],
+                        in0=gathered[g][:, :, lo - gstart[g]:lo - gstart[g] + n].rearrange("p t n -> p n t"),
+                        scalar1=1.0,
+                        scalar2=0.0,
+                        op0=mult,
+                        op1=add,
+                    )
                 lo += n
 
         def quantize(c):

@@ -67,13 +67,11 @@ def tile_routed_moe_kernel(tc, xT, w_words, w_scales, b, gate, offs, pos1, pos2,
             for r in range(4):
                 nc.sync.dma_start(w_sc[r:P:32, :, :].bitcast(I32), sc_rows[r].bitcast(I32))
 
-        w_codes = []
+        w_all = keep.tile([P, EXPERTS, FEATURES], I32, name="w_all", align_bytes=64)
+        w_codes = [w_all[:, e, :] for e in range(EXPERTS)]
 
         def load_codes():
-            for e in range(EXPERTS):
-                wc = keep.tile([P, FEATURES], I32, name="w_codes%d" % e, align_bytes=64)
-                nc.sync.dma_start(wc[:], w_words[e, 0].rearrange("p n r -> p (n r)").bitcast(I32))
-                w_codes.append(wc)
+            nc.sync.dma_start(w_all[:], w_words.rearrange("e a p n r -> p (e a) (n r)").bitcast(I32))
 
         load_scales()
         load_codes()
@@ -83,11 +81,11 @@ def tile_routed_moe_kernel(tc, xT, w_words, w_scales, b, gate, offs, pos1, pos2,
         bias_t = keep.tile([P, BLOCKS, EXPERTS], F32, name="bias_t")
         nc.sync.dma_start(bias_t[:], b.rearrange("(h p) e -> p h e", p=P))
         gates = {}
+        g_all = keep.tile([P, 2 * BLOCKS, TOKENS], F32, name="g_all")
+        nc.sync.dma_start(g_all[:], gate.rearrange("r (h p) n -> p (r h) n", p=P))
         for h in range(BLOCKS):
             for r in range(2):
-                g = keep.tile([P, TOKENS], F32, name="gate%d_%d" % (r, h))
-                nc.sync.dma_start(g[:], gate[r, h * P:(h + 1) * P, :])
-                gates[(r, h)] = g
+                gates[(r, h)] = g_all[:, r * BLOCKS + h, :]
 
         y = [keep.tile([P, SLOTS], F32, name="y%d" % h) for h in range(BLOCKS)]
         qstart = [sum(QCH[:c]) for c in range(len(QCH))]

@@ -22,8 +22,10 @@ FEATURES = 256
 BLOCKS = FEATURES // P
 PACK = 4
 QCH = [512,256,128,128]
-GCH = [256,256,256,256]
-V_EMPTIES = [4,5]
+GCH = [512,384,128]
+WINDOW = TOKENS + 16
+V_EMPTIES = []
+V_WIDE = [0]
 
 
 def tile_routed_moe_kernel(tc, xT, w_words, w_scales, b, gate, offs, pos1, pos2, out):
@@ -51,13 +53,18 @@ def tile_routed_moe_kernel(tc, xT, w_words, w_scales, b, gate, offs, pos1, pos2,
         pos2_t = lists.tile([P, TOKENS // 16], U16, name="pos2_t")
 
         x_rows = xT.rearrange("(p t) n -> t p n", t=PACK)
+        x_flat = xT.rearrange("(p t) n -> p (t n)", t=PACK)
         planes = {}
-        for i, t in enumerate([2,0,3,1]):
-            plane = keep.tile([P, TOKENS], F32, name="plane%d" % t)
-            nc.sync.dma_start(plane[:], x_rows[t])
-            planes[t] = plane
-            if i == 0:
-                nc.sync.dma_start(offs_t[:], offs)
+        planes[2] = keep.tile([P, TOKENS], F32, name="plane2")
+        nc.sync.dma_start(planes[2][:], x_rows[2])
+        nc.sync.dma_start(offs_t[:], offs)
+        planes[0] = keep.tile([P, WINDOW], F32, name="plane0")
+        nc.sync.dma_start(planes[0][:], x_flat[:, 0:WINDOW])
+        odd = keep.tile([P, 2, TOKENS], F32, name="odd")
+        nc.sync.dma_start(odd[:], xT.rearrange("(p u t) n -> t p u n", u=2, t=2)[1])
+        again = keep.tile([P, TOKENS], F32, name="again")
+        nc.sync.dma_start(again[:], x_rows[0])
+        nc.sync.dma_start(pos1_t[:], pos1)
 
         w_sc = keep.tile([P, EXPERTS, FEATURES], U8, name="w_sc", align_bytes=64)
         nc.vector.memset(w_sc[:].rearrange("p e n -> p (e n)").bitcast(I32), 0)
@@ -76,7 +83,6 @@ def tile_routed_moe_kernel(tc, xT, w_words, w_scales, b, gate, offs, pos1, pos2,
         load_scales()
         load_codes()
 
-        nc.sync.dma_start(pos1_t[:], pos1)
         nc.sync.dma_start(pos2_t[:], pos2)
         bias_t = keep.tile([P, BLOCKS, EXPERTS], F32, name="bias_t")
         nc.sync.dma_start(bias_t[:], b.rearrange("(h p) e -> p h e", p=P))
@@ -100,15 +106,21 @@ def tile_routed_moe_kernel(tc, xT, w_words, w_scales, b, gate, offs, pos1, pos2,
             return c, slot - qstart[c]
 
         xb = keep.tile([P, 2, TOKENS], BF16, name="xb")
-        nc.vector.tensor_copy(xb[:, 0, :], planes[2][:])
-        nc.gpsimd.tensor_scalar(out=xb[:, 1, :], in0=planes[3][:], scalar1=1.0, scalar2=0.0, op0=mult, op1=add)
+        HALF = TOKENS // 2
+        nc.vector.tensor_copy(xb[:, 0, 0:HALF], planes[2][:, 0:HALF])
+        nc.scalar.copy(xb[:, 0, HALF:TOKENS], planes[2][:, HALF:TOKENS])
+        nc.gpsimd.tensor_scalar(out=xb[:, 1, :], in0=odd[:, 1, :], scalar1=1.0, scalar2=0.0, op0=mult, op1=add)
 
         def gather(g):
             n = GCH[g]
             gt = ring.tile([P, 2, n], F32, name="gt")
             cols = offs_t[:, gstart[g] // 16:(gstart[g] + n) // 16]
             for t in range(2):
-                nc.vector.tensor_copy(gt[:, t, :], planes[t][:].indirect(cols))
+                if t == 0:
+                    window = (again if g > 0 else planes[0])[:]
+                else:
+                    window = odd[:].rearrange("p u n -> p (u n)")
+                nc.vector.tensor_copy(gt[:, t, :], window.indirect(cols))
             gathered[g] = gt
 
         def scalar_gather(e):
@@ -164,6 +176,16 @@ def tile_routed_moe_kernel(tc, xT, w_words, w_scales, b, gate, offs, pos1, pos2,
                 )
 
         def empty(c, h):
+            if h == 0 and c in V_WIDE:
+                k = QCH[c] // CAP
+                e0 = qstart[c] // CAP
+                nc.vector.tensor_tensor(
+                    y[h][:, e0 * CAP:(e0 + k) * CAP].rearrange("p (e n) -> p e n", e=k),
+                    banks[(h, c)][:].rearrange("p (e n) -> p e n", e=k),
+                    bias_t[:, h, e0:e0 + k].unsqueeze(2).to_broadcast([P, k, CAP]),
+                    add,
+                )
+                return
             for i in range(QCH[c] // CAP):
                 e = qstart[c] // CAP + i
                 if h == 0 and e in V_EMPTIES:

@@ -64,7 +64,6 @@ def tile_routed_moe_kernel(tc, xT, w_words, w_scales, b, gate, offs, pos1, pos2,
         nc.sync.dma_start(odd[:], xT.rearrange("(p u t) n -> t p u n", u=2, t=2)[1])
         again = keep.tile([P, TOKENS], F32, name="again")
         nc.sync.dma_start(again[:], x_rows[0])
-        nc.sync.dma_start(pos1_t[:], pos1)
 
         w_sc = keep.tile([P, EXPERTS, FEATURES], U8, name="w_sc", align_bytes=64)
         nc.vector.memset(w_sc[:].rearrange("p e n -> p (e n)").bitcast(I32), 0)
@@ -83,6 +82,7 @@ def tile_routed_moe_kernel(tc, xT, w_words, w_scales, b, gate, offs, pos1, pos2,
         load_scales()
         load_codes()
 
+        nc.sync.dma_start(pos1_t[:], pos1)
         nc.sync.dma_start(pos2_t[:], pos2)
         bias_t = keep.tile([P, BLOCKS, EXPERTS], F32, name="bias_t")
         nc.sync.dma_start(bias_t[:], b.rearrange("(h p) e -> p h e", p=P))

@@ -38,7 +38,7 @@ def tile_routed_moe_kernel(tc, xT, w_words, w_scales, b, gate, offs, pos1, pos2,
     with ExitStack() as ctx:
         lists = ctx.enter_context(tc.tile_pool(name="lists", bufs=1))
         keep = ctx.enter_context(tc.tile_pool(name="keep", bufs=1))
-        ring = ctx.enter_context(tc.tile_pool(name="ring", bufs=3))
+        ring = ctx.enter_context(tc.tile_pool(name="ring", bufs=2))
         psum = ctx.enter_context(tc.psum_pool(name="psum", bufs=1))
 
         warm = keep.tile([P, 2], F32, name="warm")
@@ -138,9 +138,10 @@ def tile_routed_moe_kernel(tc, xT, w_words, w_scales, b, gate, offs, pos1, pos2,
                 c, o = where(lo)
                 n = min(QCH[c] - o, gstart[g] + GCH[g] - lo)
                 if c in [3]:
-                    nc.vector.tensor_copy(
-                        out=grouped[c][:, o:o + n, 0:2],
-                        in_=gathered[g][:, :, lo - gstart[g]:lo - gstart[g] + n].rearrange("p t n -> p n t"),
+                    nc.scalar.activation(
+                        grouped[c][:, o:o + n, 0:2],
+                        gathered[g][:, :, lo - gstart[g]:lo - gstart[g] + n].rearrange("p t n -> p n t"),
+                        copy,
                     )
                 else:
                     nc.gpsimd.tensor_scalar(

@@ -239,6 +239,10 @@ def tile_routed_moe_kernel(tc, xT, w_words, w_scales, b, gate, offs, pos1, pos2,
         nc.scalar.copy(total[0][:, 0:PE_COLS], acc[:])
         fetch(first, 1, 0, pos1_t)
         nc.vector.tensor_tensor(total[0][:, PE_COLS:TOKENS], first[0][:, PE_COLS:TOKENS], second[0][:, PE_COLS:TOKENS], add)
-        nc.sync.dma_start(out[0:P, :], total[0][:])
-        fetch(second, 1, 1, pos2_t)
-        finish(1)
+        nc.scalar.dma_start(out[0:P, :], total[0][:])
+        CUT = 256
+        fetch(second, 1, 1, pos2_t, 0, CUT)
+        fetch(second, 1, 1, pos2_t, CUT, TOKENS)
+        nc.vector.tensor_tensor(total[1][:, 0:CUT], first[1][:, 0:CUT], second[1][:, 0:CUT], add)
+        nc.vector.tensor_tensor(total[1][:, CUT:TOKENS], first[1][:, CUT:TOKENS], second[1][:, CUT:TOKENS], add)
+        nc.sync.dma_start(out[P:2 * P, :], total[1][:])

@@ -22,7 +22,7 @@ FEATURES = 256
 BLOCKS = FEATURES // P
 PACK = 4
 QCH = [512,256,128,128]
-GCH = [512,384,128]
+GCH = [256,256,256,128,128]
 WINDOW = TOKENS + 16
 V_EMPTIES = []
 V_WIDE = [0]
@@ -38,7 +38,7 @@ def tile_routed_moe_kernel(tc, xT, w_words, w_scales, b, gate, offs, pos1, pos2,
     with ExitStack() as ctx:
         lists = ctx.enter_context(tc.tile_pool(name="lists", bufs=1))
         keep = ctx.enter_context(tc.tile_pool(name="keep", bufs=1))
-        ring = ctx.enter_context(tc.tile_pool(name="ring", bufs=2))
+        ring = ctx.enter_context(tc.tile_pool(name="ring", bufs=3))
         psum = ctx.enter_context(tc.psum_pool(name="psum", bufs=1))
 
         warm = keep.tile([P, 2], F32, name="warm")
@@ -117,7 +117,7 @@ def tile_routed_moe_kernel(tc, xT, w_words, w_scales, b, gate, offs, pos1, pos2,
             cols = offs_t[:, gstart[g] // 16:(gstart[g] + n) // 16]
             for t in range(2):
                 if t == 0:
-                    window = (again if g > 0 else planes[0])[:]
+                    window = (again if g > 1 else planes[0])[:]
                 else:
                     window = odd[:].rearrange("p u n -> p (u n)")
                 nc.vector.tensor_copy(gt[:, t, :], window.indirect(cols))

@@ -22,7 +22,8 @@ FEATURES = 256
 BLOCKS = FEATURES // P
 PACK = 4
 QCH = [512,256,128,128]
-GCH = [256,256,256,128,128]
+GCH = [512,256,128,128]
+SUB = 256
 WINDOW = TOKENS + 16
 V_EMPTIES = []
 V_WIDE = [0]
@@ -115,12 +116,13 @@ def tile_routed_moe_kernel(tc, xT, w_words, w_scales, b, gate, offs, pos1, pos2,
             n = GCH[g]
             gt = ring.tile([P, 2, n], F32, name="gt")
             cols = offs_t[:, gstart[g] // 16:(gstart[g] + n) // 16]
-            for t in range(2):
-                if t == 0:
-                    window = (again if g > 1 else planes[0])[:]
-                else:
-                    window = odd[:].rearrange("p u n -> p (u n)")
-                nc.vector.tensor_copy(gt[:, t, :], window.indirect(cols))
+            nc.vector.tensor_copy(gt[:, 0, :], (again if g > 0 else planes[0])[:].indirect(cols))
+            for lo in range(0, n, SUB):
+                hi = min(n, lo + SUB)
+                nc.vector.tensor_copy(
+                    gt[:, 1, lo:hi],
+                    odd[:].rearrange("p u n -> p (u n)").indirect(offs_t[:, (gstart[g] + lo) // 16:(gstart[g] + hi) // 16]),
+                )
             gathered[g] = gt
 
         def scalar_gather(e):
@@ -136,7 +138,7 @@ def tile_routed_moe_kernel(tc, xT, w_words, w_scales, b, gate, offs, pos1, pos2,
             lo = gstart[g]
             while lo < gstart[g] + GCH[g]:
                 c, o = where(lo)
-                n = min(QCH[c] - o, gstart[g] + GCH[g] - lo)
+                n = min(QCH[c] - o, gstart[g] + GCH[g] - lo, SUB)
                 if c in [3]:
                     nc.scalar.activation(
                         grouped[c][:, o:o + n, 0:2],

@@ -100,7 +100,8 @@ def tile_routed_moe_kernel(tc, xT, w_words, w_scales, b, gate, offs, pos1, pos2,
         gathered = {}
         codes = {}
         banks = {}
-        grouped = [keep.tile([P, QCH[c], PACK], BF16, name="grouped%d" % c, align_bytes=64) for c in range(len(QCH))]
+        grouped = [keep.tile([P, QCH[c], PACK], BF16, name="grouped%d" % c, align_bytes=64) for c in range(len(QCH) - 1)]
+        last = keep.tile([P, 3, CAP], F32, name="last")
 
         def where(slot):
             c = max(i for i in range(len(QCH)) if qstart[i] <= slot)
@@ -111,10 +112,11 @@ def tile_routed_moe_kernel(tc, xT, w_words, w_scales, b, gate, offs, pos1, pos2,
         nc.vector.tensor_copy(xb[:, 0, 0:HALF], planes[2][:, 0:HALF])
         nc.scalar.copy(xb[:, 0, HALF:TOKENS], planes[2][:, HALF:TOKENS])
         nc.gpsimd.tensor_scalar(out=xb[:, 1, :], in0=odd[:, 1, :], scalar1=1.0, scalar2=0.0, op0=mult, op1=add)
+        nc.vector.tensor_copy(last[:, 2, :], planes[2][:].indirect(offs_t[:, (SLOTS - CAP) // 16:SLOTS // 16]))
 
         def gather(g):
             n = GCH[g]
-            gt = ring.tile([P, 2, n], F32, name="gt")
+            gt = last if g == len(GCH) - 1 else ring.tile([P, 2, n], F32, name="gt", align_bytes=64)
             cols = offs_t[:, gstart[g] // 16:(gstart[g] + n) // 16]
             nc.vector.tensor_copy(gt[:, 0, :], (again if g > 0 else planes[0])[:].indirect(cols))
             for lo in range(0, n, SUB):
@@ -127,7 +129,7 @@ def tile_routed_moe_kernel(tc, xT, w_words, w_scales, b, gate, offs, pos1, pos2,
 
         def scalar_gather(e):
             c, o = where(e * CAP)
-            for t in (2, 3):
+            for t in ((3,) if e == EXPERTS - 1 else (2, 3)):
                 nc.scalar.activation(
                     grouped[c][:, o:o + CAP, t],
                     xb[:, t - 2, :].indirect(offs_t[:, e * (CAP // 16):(e + 1) * (CAP // 16)]),
@@ -141,7 +143,7 @@ def tile_routed_moe_kernel(tc, xT, w_words, w_scales, b, gate, offs, pos1, pos2,
                 n = min(QCH[c] - o, gstart[g] + GCH[g] - lo, SUB)
                 if c in [3]:
                     nc.scalar.activation(
-                        grouped[c][:, o:o + n, 0:2],
+                        grouped[c][:, o:o + n, 0:3],
                         gathered[g][:, :, lo - gstart[g]:lo - gstart[g] + n].rearrange("p t n -> p n t"),
                         copy,
                     )
@@ -208,11 +210,15 @@ def tile_routed_moe_kernel(tc, xT, w_words, w_scales, b, gate, offs, pos1, pos2,
                         scale=1.0,
                     )
 
-        for e in range(EXPERTS):
+        for e in range(EXPERTS - 1):
             scalar_gather(e)
-        for g in range(len(GCH)):
+        for g in range(len(GCH) - 1):
             gather(g)
             interleave(g)
+        grouped.append(ring.tile([P, CAP, PACK], BF16, name="gt", align_bytes=64))
+        scalar_gather(EXPERTS - 1)
+        gather(len(GCH) - 1)
+        interleave(len(GCH) - 1)
         for c in range(len(QCH)):
             quantize(c)
             multiply(c, 0)

@@ -39,7 +39,7 @@ def tile_routed_moe_kernel(tc, xT, w_words, w_scales, b, gate, offs, pos1, pos2,
     with ExitStack() as ctx:
         lists = ctx.enter_context(tc.tile_pool(name="lists", bufs=1))
         keep = ctx.enter_context(tc.tile_pool(name="keep", bufs=1))
-        ring = ctx.enter_context(tc.tile_pool(name="ring", bufs=3))
+        ring = ctx.enter_context(tc.tile_pool(name="ring", bufs=2))
         psum = ctx.enter_context(tc.psum_pool(name="psum", bufs=1))
 
         warm = keep.tile([P, 2], F32, name="warm")
@@ -148,14 +148,21 @@ def tile_routed_moe_kernel(tc, xT, w_words, w_scales, b, gate, offs, pos1, pos2,
                         copy,
                     )
                 else:
+                    m = n // 2 if c == len(QCH) - 2 else n
                     nc.gpsimd.tensor_scalar(
-                        out=grouped[c][:, o:o + n, 0:2],
-                        in0=gathered[g][:, :, lo - gstart[g]:lo - gstart[g] + n].rearrange("p t n -> p n t"),
+                        out=grouped[c][:, o:o + m, 0:2],
+                        in0=gathered[g][:, :, lo - gstart[g]:lo - gstart[g] + m].rearrange("p t n -> p n t"),
                         scalar1=1.0,
                         scalar2=0.0,
                         op0=mult,
                         op1=add,
                     )
+                    if m < n:
+                        nc.scalar.activation(
+                            grouped[c][:, o + m:o + n, 0:2],
+                            gathered[g][:, :, lo - gstart[g] + m:lo - gstart[g] + n].rearrange("p t n -> p n t"),
+                            copy,
+                        )
                 lo += n
 
         def quantize(c):

@@ -63,8 +63,6 @@ def tile_routed_moe_kernel(tc, xT, w_words, w_scales, b, gate, offs, pos1, pos2,
         nc.sync.dma_start(planes[0][:], x_flat[:, 0:WINDOW])
         odd = keep.tile([P, 2, TOKENS], F32, name="odd")
         nc.sync.dma_start(odd[:], xT.rearrange("(p u t) n -> t p u n", u=2, t=2)[1])
-        again = keep.tile([P, TOKENS], F32, name="again")
-        nc.sync.dma_start(again[:], x_rows[0])
 
         w_sc = keep.tile([P, EXPERTS, FEATURES], U8, name="w_sc", align_bytes=64)
         nc.vector.memset(w_sc[:].rearrange("p e n -> p (e n)").bitcast(I32), 0)
@@ -111,14 +109,16 @@ def tile_routed_moe_kernel(tc, xT, w_words, w_scales, b, gate, offs, pos1, pos2,
         HALF = TOKENS // 2
         nc.vector.tensor_copy(xb[:, 0, 0:HALF], planes[2][:, 0:HALF])
         nc.scalar.copy(xb[:, 0, HALF:TOKENS], planes[2][:, HALF:TOKENS])
-        nc.gpsimd.tensor_scalar(out=xb[:, 1, :], in0=odd[:, 1, :], scalar1=1.0, scalar2=0.0, op0=mult, op1=add)
+        hold = ring.tile([P, 1], F32, name="gt", align_bytes=64)
+        nc.gpsimd.memset(hold[:], 0.0)
+        nc.gpsimd.tensor_scalar(out=xb[:, 1, :], in0=odd[:, 1, :], scalar1=1.0, scalar2=hold[:, 0:1], op0=mult, op1=add)
         nc.vector.tensor_copy(last[:, 2, :], planes[2][:].indirect(offs_t[:, (SLOTS - CAP) // 16:SLOTS // 16]))
 
         def gather(g):
             n = GCH[g]
             gt = last if g == len(GCH) - 1 else ring.tile([P, 2, n], F32, name="gt", align_bytes=64)
             cols = offs_t[:, gstart[g] // 16:(gstart[g] + n) // 16]
-            nc.vector.tensor_copy(gt[:, 0, :], (again if g > 0 else planes[0])[:].indirect(cols))
+            nc.vector.tensor_copy(gt[:, 0, :], planes[0][:].indirect(cols))
             for lo in range(0, n, SUB):
                 hi = min(n, lo + SUB)
                 nc.vector.tensor_copy(
@@ -259,5 +259,6 @@ def tile_routed_moe_kernel(tc, xT, w_words, w_scales, b, gate, offs, pos1, pos2,
         fetch(second, 1, 1, pos2_t, 0, CUT)
         fetch(second, 1, 1, pos2_t, CUT, TOKENS)
         nc.vector.tensor_tensor(total[1][:, 0:CUT], first[1][:, 0:CUT], second[1][:, 0:CUT], add)
+        nc.sync.dma_start(out[P:2 * P, 0:CUT], total[1][:, 0:CUT])
         nc.vector.tensor_tensor(total[1][:, CUT:TOKENS], first[1][:, CUT:TOKENS], second[1][:, CUT:TOKENS], add)
-        nc.sync.dma_start(out[P:2 * P, :], total[1][:])
+        nc.sync.dma_start(out[P:2 * P, CUT:TOKENS], total[1][:, CUT:TOKENS])

@@ -86,11 +86,11 @@ def tile_routed_moe_kernel(tc, xT, w_words, w_scales, b, gate, offs, pos1, pos2,
         bias_t = keep.tile([P, BLOCKS, EXPERTS], F32, name="bias_t")
         nc.sync.dma_start(bias_t[:], b.rearrange("(h p) e -> p h e", p=P))
         gates = {}
-        g_all = keep.tile([P, 2 * BLOCKS, TOKENS], F32, name="g_all")
-        nc.sync.dma_start(g_all[:], gate.rearrange("r (h p) n -> p (r h) n", p=P))
+        g_all = keep.tile([P, 2, TOKENS], F32, name="g_all")
+        nc.sync.dma_start(g_all[:], gate[:, 0:P, :].rearrange("r p n -> p r n"))
         for h in range(BLOCKS):
             for r in range(2):
-                gates[(r, h)] = g_all[:, r * BLOCKS + h, :]
+                gates[(r, h)] = g_all[:, r, :]
 
         y = [keep.tile([P, SLOTS], F32, name="y%d" % h) for h in range(BLOCKS)]
         qstart = [sum(QCH[:c]) for c in range(len(QCH))]

from contextlib import ExitStack

import concourse.mybir as mybir
from concourse.masks import make_identity

FLOPS = 2 * 512 * 256 * 1024

F32 = mybir.dt.float32
BF16 = mybir.dt.bfloat16
U32 = mybir.dt.uint32
I32 = mybir.dt.int32
U16 = mybir.dt.uint16
U8 = mybir.dt.uint8
FP8X4 = mybir.dt.float8_e4m3fn_x4

P = 128
TOKENS = 512
EXPERTS = 8
CAP = 128
SLOTS = EXPERTS * CAP
FEATURES = 256
BLOCKS = FEATURES // P
PACK = 4
QCH = [512,256,128,128]
GCH = [512,256,128,128]
SUB = 256
WINDOW = TOKENS + 16
V_EMPTIES = []
V_WIDE = [0]


def tile_routed_moe_kernel(tc, xT, w_words, w_scales, b, gate, offs, pos1, pos2, out):
    nc = tc.nc
    mult = mybir.AluOpType.mult
    add = mybir.AluOpType.add
    identity = mybir.ActivationFunctionType.Identity
    copy = mybir.ActivationFunctionType.Copy

    with ExitStack() as ctx:
        lists = ctx.enter_context(tc.tile_pool(name="lists", bufs=1))
        keep = ctx.enter_context(tc.tile_pool(name="keep", bufs=1))
        ring = ctx.enter_context(tc.tile_pool(name="ring", bufs=2))
        psum = ctx.enter_context(tc.psum_pool(name="psum", bufs=1))

        warm = keep.tile([P, 2], F32, name="warm")
        nc.vector.memset(warm[:, 0:1], 0.0)
        nc.scalar.activation(out=warm[:, 1:2], in_=warm[:, 0:1], func=copy)

        ident = keep.tile([P, P], F32, name="ident")
        make_identity(nc, ident[:])

        offs_t = lists.tile([P, SLOTS // 16], U16, name="offs_t")
        pos1_t = lists.tile([P, TOKENS // 16], U16, name="pos1_t")
        pos2_t = lists.tile([P, TOKENS // 16], U16, name="pos2_t")

        x_rows = xT.rearrange("(p t) n -> t p n", t=PACK)
        x_flat = xT.rearrange("(p t) n -> p (t n)", t=PACK)
        planes = {}
        planes[2] = keep.tile([P, TOKENS], F32, name="plane2")
        nc.sync.dma_start(planes[2][:], x_rows[2])
        nc.sync.dma_start(offs_t[:], offs)
        planes[0] = keep.tile([P, WINDOW], F32, name="plane0")
        nc.sync.dma_start(planes[0][:], x_flat[:, 0:WINDOW])
        odd = keep.tile([P, 2, TOKENS], F32, name="odd")
        nc.sync.dma_start(odd[:], xT.rearrange("(p u t) n -> t p u n", u=2, t=2)[1])

        w_sc = keep.tile([P, EXPERTS, FEATURES], U8, name="w_sc", align_bytes=64)
        nc.vector.memset(w_sc[:].rearrange("p e n -> p (e n)").bitcast(I32), 0)
        sc_rows = w_scales.rearrange("e a (q r) n -> r q (e a) n", r=4)

        def load_scales():
            for r in range(4):
                nc.sync.dma_start(w_sc[r:P:32, :, :].bitcast(I32), sc_rows[r].bitcast(I32))

        w_all = keep.tile([P, EXPERTS, FEATURES], I32, name="w_all", align_bytes=64)
        w_codes = [w_all[:, e, :] for e in range(EXPERTS)]

        def load_codes():
            nc.sync.dma_start(w_all[:], w_words.rearrange("e a p n r -> p (e a) (n r)").bitcast(I32))

        load_scales()
        load_codes()

        nc.sync.dma_start(pos1_t[:], pos1)
        nc.sync.dma_start(pos2_t[:], pos2)
        bias_t = keep.tile([P, BLOCKS, EXPERTS], F32, name="bias_t")
        nc.sync.dma_start(bias_t[:], b.rearrange("(h p) e -> p h e", p=P))
        gates = {}
        g_all = keep.tile([P, 2, TOKENS], F32, name="g_all")
        nc.sync.dma_start(g_all[:], gate[:, 0:P, :].rearrange("r p n -> p r n"))
        for h in range(BLOCKS):
            for r in range(2):
                gates[(r, h)] = g_all[:, r, :]

        y = [keep.tile([P, SLOTS], F32, name="y%d" % h) for h in range(BLOCKS)]
        qstart = [sum(QCH[:c]) for c in range(len(QCH))]
        gstart = [sum(GCH[:c]) for c in range(len(GCH))]
        gathered = {}
        codes = {}
        banks = {}
        grouped = [keep.tile([P, QCH[c], PACK], BF16, name="grouped%d" % c, align_bytes=64) for c in range(len(QCH) - 1)]
        last = keep.tile([P, 3, CAP], F32, name="last")

        def where(slot):
            c = max(i for i in range(len(QCH)) if qstart[i] <= slot)
            return c, slot - qstart[c]

        xb = keep.tile([P, 2, TOKENS], BF16, name="xb")
        HALF = TOKENS // 2
        nc.vector.tensor_copy(xb[:, 0, 0:HALF], planes[2][:, 0:HALF])
        nc.scalar.copy(xb[:, 0, HALF:TOKENS], planes[2][:, HALF:TOKENS])
        hold = ring.tile([P, 1], F32, name="gt", align_bytes=64)
        nc.gpsimd.memset(hold[:], 0.0)
        nc.gpsimd.tensor_scalar(out=xb[:, 1, :], in0=odd[:, 1, :], scalar1=1.0, scalar2=hold[:, 0:1], op0=mult, op1=add)
        nc.vector.tensor_copy(last[:, 2, :], planes[2][:].indirect(offs_t[:, (SLOTS - CAP) // 16:SLOTS // 16]))

        def gather(g):
            n = GCH[g]
            gt = last if g == len(GCH) - 1 else ring.tile([P, 2, n], F32, name="gt", align_bytes=64)
            cols = offs_t[:, gstart[g] // 16:(gstart[g] + n) // 16]
            nc.vector.tensor_copy(gt[:, 0, :], planes[0][:].indirect(cols))
            for lo in range(0, n, SUB):
                hi = min(n, lo + SUB)
                nc.vector.tensor_copy(
                    gt[:, 1, lo:hi],
                    odd[:].rearrange("p u n -> p (u n)").indirect(offs_t[:, (gstart[g] + lo) // 16:(gstart[g] + hi) // 16]),
                )
            gathered[g] = gt

        def scalar_gather(e):
            c, o = where(e * CAP)
            for t in ((3,) if e == EXPERTS - 1 else (2, 3)):
                nc.scalar.activation(
                    grouped[c][:, o:o + CAP, t],
                    xb[:, t - 2, :].indirect(offs_t[:, e * (CAP // 16):(e + 1) * (CAP // 16)]),
                    copy,
                )

        def interleave(g):
            lo = gstart[g]
            while lo < gstart[g] + GCH[g]:
                c, o = where(lo)
                n = min(QCH[c] - o, gstart[g] + GCH[g] - lo, SUB)
                if c in [3]:
                    nc.scalar.activation(
                        grouped[c][:, o:o + n, 0:3],
                        gathered[g][:, :, lo - gstart[g]:lo - gstart[g] + n].rearrange("p t n -> p n t"),
                        copy,
                    )
                else:
                    m = n // 2 if c == len(QCH) - 2 else n
                    nc.gpsimd.tensor_scalar(
                        out=grouped[c][:, o:o + m, 0:2],
                        in0=gathered[g][:, :, lo - gstart[g]:lo - gstart[g] + m].rearrange("p t n -> p n t"),
                        scalar1=1.0,
                        scalar2=0.0,
                        op0=mult,
                        op1=add,
                    )
                    if m < n:
                        nc.scalar.activation(
                            grouped[c][:, o + m:o + n, 0:2],
                            gathered[g][:, :, lo - gstart[g] + m:lo - gstart[g] + n].rearrange("p t n -> p n t"),
                            copy,
                        )
                lo += n

        def quantize(c):
            n = QCH[c]
            xc = keep.tile([P, n], U32, name="x_codes%d" % c, align_bytes=64)
            xs = keep.tile([P, n], U8, name="x_sc%d" % c, align_bytes=64)
            nc.vector.quantize_mx(out=xc[:].bitcast(FP8X4), scales=xs[:], in_=grouped[c][:].rearrange("p n t -> p (n t)"))
            codes[c] = (xc, xs)

        def multiply(c, h):
            xc, xs = codes[c]
            banks[(h, c)] = psum.tile([P, QCH[c]], F32, name="bank%d" % c)
            for i in range(QCH[c] // CAP):
                e = qstart[c] // CAP + i
                nc.tensor.matmul_mx(
                    out=banks[(h, c)][:, i * CAP:(i + 1) * CAP],
                    lhsT=w_codes[e][:, h * P:(h + 1) * P].bitcast(FP8X4),
                    lhsT_scale=w_sc[:, e, h * P:(h + 1) * P],
                    rhs=xc[:, i * CAP:(i + 1) * CAP].bitcast(FP8X4),
                    rhs_scale=xs[:, i * CAP:(i + 1) * CAP],
                    start=True,
                    stop=True,
                )

        def empty(c, h):
            if h == 0 and c in V_WIDE:
                k = QCH[c] // CAP
                e0 = qstart[c] // CAP
                nc.vector.tensor_tensor(
                    y[h][:, e0 * CAP:(e0 + k) * CAP].rearrange("p (e n) -> p e n", e=k),
                    banks[(h, c)][:].rearrange("p (e n) -> p e n", e=k),
                    bias_t[:, h, e0:e0 + k].unsqueeze(2).to_broadcast([P, k, CAP]),
                    add,
                )
                return
            for i in range(QCH[c] // CAP):
                e = qstart[c] // CAP + i
                if h == 0 and e in V_EMPTIES:
                    nc.vector.tensor_scalar(
                        out=y[h][:, e * CAP:(e + 1) * CAP],
                        in0=banks[(h, c)][:, i * CAP:(i + 1) * CAP],
                        scalar1=bias_t[:, h, e:e + 1],
                        scalar2=None,
                        op0=add,
                    )
                else:
                    nc.scalar.activation(
                        out=y[h][:, e * CAP:(e + 1) * CAP],
                        in_=banks[(h, c)][:, i * CAP:(i + 1) * CAP],
                        func=identity,
                        bias=bias_t[:, h, e:e + 1],
                        scale=1.0,
                    )

        for e in range(EXPERTS - 1):
            scalar_gather(e)
        for g in range(len(GCH) - 1):
            gather(g)
            interleave(g)
        grouped.append(ring.tile([P, CAP, PACK], BF16, name="gt", align_bytes=64))
        scalar_gather(EXPERTS - 1)
        gather(len(GCH) - 1)
        interleave(len(GCH) - 1)
        for c in range(len(QCH)):
            quantize(c)
            multiply(c, 0)
            empty(c, 0)
        for c in range(len(QCH)):
            multiply(c, 1)
            empty(c, 1)

        first = [keep.tile([P, TOKENS], F32, name="first%d" % h) for h in range(BLOCKS)]
        second = [keep.tile([P, TOKENS], F32, name="second%d" % h) for h in range(BLOCKS)]
        total = [keep.tile([P, TOKENS], F32, name="total%d" % h) for h in range(BLOCKS)]

        def fetch(dst, h, r, pos_t, lo=0, hi=TOKENS):
            nc.vector.tensor_tensor(dst[h][:, lo:hi], y[h][:].indirect(pos_t[:, lo // 16:hi // 16]), gates[(r, h)][:, lo:hi], mult)

        def finish(h, lo=0, hi=TOKENS):
            nc.vector.tensor_tensor(total[h][:, lo:hi], first[h][:, lo:hi], second[h][:, lo:hi], add)
            nc.sync.dma_start(out[h * P:(h + 1) * P, lo:hi], total[h][:, lo:hi])

        PE_COLS = 400
        acc = psum.tile([P, PE_COLS], F32, name="acc")
        fetch(first, 0, 0, pos1_t)
        nc.tensor.matmul(acc[:], lhsT=ident[:], rhs=first[0][:, 0:PE_COLS], start=True, stop=False)
        fetch(second, 0, 1, pos2_t)
        nc.tensor.matmul(acc[:], lhsT=ident[:], rhs=second[0][:, 0:PE_COLS], start=False, stop=True)
        nc.scalar.copy(total[0][:, 0:PE_COLS], acc[:])
        fetch(first, 1, 0, pos1_t)
        nc.vector.tensor_tensor(total[0][:, PE_COLS:TOKENS], first[0][:, PE_COLS:TOKENS], second[0][:, PE_COLS:TOKENS], add)
        nc.scalar.dma_start(out[0:P, :], total[0][:])
        CUT = 256
        fetch(second, 1, 1, pos2_t, 0, CUT)
        fetch(second, 1, 1, pos2_t, CUT, TOKENS)
        nc.vector.tensor_tensor(total[1][:, 0:CUT], first[1][:, 0:CUT], second[1][:, 0:CUT], add)
        nc.sync.dma_start(out[P:2 * P, 0:CUT], total[1][:, 0:CUT])
        nc.vector.tensor_tensor(total[1][:, CUT:TOKENS], first[1][:, CUT:TOKENS], second[1][:, CUT:TOKENS], add)
        nc.sync.dma_start(out[P:2 * P, CUT:TOKENS], total[1][:, CUT:TOKENS])
